import numpy as np, ml_dtypes
CORES = [35,38,43,46]
N = 4
import mx_ref
NC, G = 256, 2
C = np.float32(0.019)
BF = ml_dtypes.bfloat16
def cut(t, i, w=512):
    return t[:, w * i:w * i + w]
def tile(rs):
    return np.stack(rs, axis=2).reshape(128, -1).astype(BF)
def layer(w, X):
    out = []
    for i in range(G):
        for t in range(len(X)):
            p = mx_ref.matmul(mx_ref.quantize(cut(w, len(X) * i + t)), X[t])
            z = p if t == 0 else z + p
        out.append(z)
    return out
def masked(A, E):
    return [(e * (s * a > 0)) * C for a, e in zip(A, E) for s in (1, -1)]
def setup_inputs(rng):
    def f(*shape):
        return mx_ref.flush((rng.standard_normal(shape, dtype=np.float32) * np.exp2(rng.integers(-2, 3, shape[:-1] + (1,)))).astype(BF))
    return {"x": f(N, 128, 512), "e": f(N, 128, 512), "a": f(N, 128, G * 512), "w": f(N, 128, 512), "v": f(N, 128, 4 * NC)}
def setup_inputs_blocks(rng):
    d = setup_inputs(rng)
    for k in ("x", "e", "a", "w", "v"): d[k] = mx_ref.spread(d[k], rng, 4)
    return d
def setup_inputs_wide(rng):
    d = setup_inputs(rng)
    for k in ("x", "e", "a", "w", "v"): d[k] = mx_ref.flush((d[k].astype(np.float32) * np.exp2(rng.integers(-6, 7, (N, 1, 1))).astype(np.float32)).astype(BF))
    return d
def setup_inputs_zeros(rng):
    d = setup_inputs(rng); v = d["x"].reshape(N, 128, -1, 4).copy()
    v[np.broadcast_to((rng.random((N, 1, v.shape[2], 1)) < 0.33), v.shape)] = 0
    d["x"] = v.reshape(d["x"].shape)
    return d
def reference(x, e, a, w, v):
    T = [mx_ref.quantize(tile(masked(layer(a[j], [mx_ref.quantize(x[j])]), layer(a[j], [mx_ref.quantize(e[j])])))) for j in range(N)]
    y = np.zeros((N, 128, N * 128), np.float32); z = np.zeros((N, 128, N * NC), np.float32)
    for r in range(N):
        qw = mx_ref.quantize(w[r]); qv = mx_ref.quantize(v[r])
        for j in range(N):
            y[r][:, 128 * j:128 * j + 128] = mx_ref.matmul(qw, T[j])
            p = mx_ref.matmul(T[j], qv)
            z[r][:, NC * j:NC * j + NC] = p
    return {"y": y, "z": z}

@@ -1,0 +1,165 @@
+from concourse.bass import DstId, RemoteDMATransfer
+from concourse.mybir import dt, AluOpType, ActivationFunctionType
+
+C = 0.019
+N, COLS, NC = 4, 128, 256
+
+SCRATCH = {
+    "xb": ("sbuf", [128, 512], "bfloat16"),
+    "eb": ("sbuf", [128, 512], "bfloat16"),
+    "ab": ("sbuf", [128, 1024], "bfloat16"),
+    "wb": ("sbuf", [128, 512], "bfloat16"),
+    "vb": ("sbuf", [128, 1024], "bfloat16"),
+    "tb": ("sbuf", [128, 512], "bfloat16"),
+    "xq": ("sbuf", [128, 128], "float8_e4m3fn_x4"), "xs": ("sbuf", [128, 128], "uint8"),
+    "eq": ("sbuf", [128, 128], "float8_e4m3fn_x4"), "es": ("sbuf", [128, 128], "uint8"),
+    "aq": ("sbuf", [128, 256], "float8_e4m3fn_x4"), "as_": ("sbuf", [128, 256], "uint8"),
+    "wq": ("sbuf", [128, 128], "float8_e4m3fn_x4"), "ws": ("sbuf", [128, 128], "uint8"),
+    "vq": ("sbuf", [128, 256], "float8_e4m3fn_x4"), "vs": ("sbuf", [128, 256], "uint8"),
+    "q": ("sbuf", [128, N * COLS], "float8_e4m3fn_x4"), "s": ("sbuf", [128, N * COLS], "uint8"),
+    "m0": ("sbuf", [128, 128], "float32"), "m1": ("sbuf", [128, 128], "float32"),
+    "m2": ("sbuf", [128, 128], "float32"), "m3": ("sbuf", [128, 128], "float32"),
+    "yb": ("sbuf", [128, N * COLS], "float32"),
+    "zb": ("sbuf", [128, N * NC], "float32"),
+    "ps": ("psum", [128, 512 * 8], "float32"),
+}
+SEMAPHORES = (["ld_" + k for k in "xeawv"] + ["q_" + k for k in "xeawvt"] + ["u0", "u1", "d0", "d1", "k0", "k1", "k2", "k3", "res"]
+              + ["py%d" % j for j in range(N)] + ["pz%d" % j for j in range(N)]
+              + ["cy%d" % j for j in range(N)] + ["cz%d" % j for j in range(N)]
+              + ["arr%d" % j for j in range(N)] + ["sent", "stored"])
+
+
+def engines(mask, n):
+    bits = [b for b in range(mask.bit_length()) if mask >> b & 1]
+    step = len(bits) // n
+    return sum(1 << b for b in bits[::step][:n])
+
+
+def rank_program(g, core, T, topo):
+    me = T.rank_of(core)
+    if me is None:
+        return
+    sem = T.sem
+    copy = ActivationFunctionType.Copy
+    near = [r for r in range(N) if r != me and topo.chip(T.cores[r]) == topo.chip(core)][0]
+    far = [r for r in range(N) if topo.chip(T.cores[r]) != topo.chip(core)]
+    far = sorted(far, key=lambda r: topo.die(T.cores[r]) != topo.die(core))
+    f1, f2 = far
+    lo, hi = min(far), max(far) + 1
+    off = topo.mask(core, T.cores[f1])
+    inner = topo.mask(core, T.cores[near]) & ~off
+    n_off, n_in = 8, 4
+    m_off, m_in = engines(off, n_off), engines(inner, n_in)
+
+    def cols(j, w=COLS):
+        return slice(w * j, w * j + w)
+
+    def bank(k, n):
+        return T.ps[:, 512 * k:512 * k + n]
+
+    g.scalar.dma_start(T.ab[:], T.a[:]).then_inc(sem.ld_a, 16)
+    for k in "xewv":
+        g.sync.dma_start(T[k + "b"][:], T[k][:]).then_inc(sem["ld_" + k], 16)
+
+    v = g.vector
+
+    def quant(k, plane):
+        v.wait_ge(sem["ld_" + k], 16)
+        v.quantize_mx(T[k + "q"][:], T[plane][:], T[k + "b"][:]).then_inc(sem["q_" + k], 1)
+
+    def masks(i):
+        v.wait_ge(sem["u%d" % i], 1)
+        for h, op in enumerate((AluOpType.is_gt, AluOpType.is_lt)):
+            b = 2 * i + h
+            v.tensor_scalar(T["m%d" % b][:], bank(i, COLS), 0.0, C, op, AluOpType.mult).then_inc(sem["k%d" % b], 1)
+
+    quant("x", "xs")
+    quant("a", "as_")
+    masks(0)
+    quant("e", "es")
+    masks(1)
+    for i in range(2):
+        v.wait_ge(sem["d%d" % i], 1)
+        for b in (2 * i, 2 * i + 1):
+            v.wait_ge(sem["k%d" % b], 1)
+            v.tensor_tensor(T.tb[:, b:4 * COLS:4], T["m%d" % b][:], bank(2 + i, COLS), AluOpType.mult).then_inc(sem.res, 1)
+    v.wait_ge(sem.res, 4)
+    v.quantize_mx(T.q[:, cols(me)], T.s[:, cols(me)], T.tb[:]).then_inc(sem.q_t, 1)
+    quant("w", "ws")
+    quant("v", "vs")
+
+    g.wait_ge(sem.q_t, 1)
+
+    def dst(r):
+        rid, pnc, _ = topo.addr(T.cores[r])
+        return DstId(rid=rid, pnc=pnc)
+
+    arr = sem["arr%d" % me]
+    for part in (T.q[:, cols(me)].bitcast(dt.uint8), T.s[:, cols(me)]):
+        g.remote_dma_fused([
+            RemoteDMATransfer(dst_ids=[dst(f1), dst(f2)], dma_engine_mask=m_off, remote_sem=arr, srcs=[part], dsts=[part, part]),
+            RemoteDMATransfer(dst_ids=[dst(near)], dma_engine_mask=m_in, remote_sem=arr, srcs=[part], dsts=[part]),
+        ], local_sem=sem.sent)
+    g.wait_ge(sem.sent, 2 * (n_off + n_in))
+
+    t = g.tensor
+
+    def yprod(j, k):
+        t.matmul_mx(bank(k, COLS), T.wq[:], T.ws[:], T.q[:, cols(j)], T.s[:, cols(j)], True, True).then_inc(sem["py%d" % j], 1)
+
+    def zprod(j, k):
+        t.matmul_mx(bank(k, NC), T.q[:, cols(j)], T.s[:, cols(j)], T.vq[:], T.vs[:], True, True).then_inc(sem["pz%d" % j], 1)
+
+    t.wait_ge(sem.q_x, 1)
+    t.wait_ge(sem.q_a, 1)
+    for i in range(2):
+        t.matmul_mx(bank(i, COLS), T.aq[:, cols(i)], T.as_[:, cols(i)], T.xq[:], T.xs[:], True, True).then_inc(sem["u%d" % i], 1)
+    t.wait_ge(sem.q_e, 1)
+    for i in range(2):
+        t.matmul_mx(bank(2 + i, COLS), T.aq[:, cols(i)], T.as_[:, cols(i)], T.eq[:], T.es[:], True, True).then_inc(sem["d%d" % i], 1)
+    ybank = {me: 4, near: 6, f1: 0, f2: 2}
+    zbank = {me: 5, near: 7, f1: 1, f2: 3}
+    t.wait_ge(sem.q_t, 1)
+    t.wait_ge(sem.q_w, 1)
+    yprod(me, ybank[me])
+    t.wait_ge(sem.q_v, 1)
+    zprod(me, zbank[me])
+    t.wait_ge(sem["arr%d" % near], 2 * n_in)
+    zprod(near, zbank[near])
+    yprod(near, ybank[near])
+    for j in far:
+        t.wait_ge(sem["arr%d" % j], 2 * n_off)
+        zprod(j, zbank[j])
+    for j in far:
+        yprod(j, ybank[j])
+
+    def out_v(kind, j, k, w):
+        v.wait_ge(sem["p%s%d" % (kind, j)], 1)
+        v.tensor_copy(T[kind + "b"][:, cols(j, w)], bank(k, w)).then_inc(sem["c%s%d" % (kind, j)], 1)
+
+    def out_s(kind, j, k, w):
+        g.scalar.wait_ge(sem["p%s%d" % (kind, j)], 1)
+        g.scalar.activation(T[kind + "b"][:, cols(j, w)], bank(k, w), copy).then_inc(sem["c%s%d" % (kind, j)], 1)
+
+    out_v("y", me, ybank[me], COLS)
+    out_s("z", me, zbank[me], NC)
+    out_v("z", near, zbank[near], NC)
+    out_s("y", near, ybank[near], COLS)
+    out_v("z", f1, zbank[f1], NC)
+    out_s("z", f2, zbank[f2], NC)
+    out_v("y", f1, ybank[f1], COLS)
+    out_s("y", f2, ybank[f2], COLS)
+
+    def store(queue, kind, js, w):
+        for j in js:
+            queue.wait_ge(sem["c%s%d" % (kind, j)], 1)
+        a, b = w * min(js), w * (max(js) + 1)
+        queue.dma_start(T[kind][:, a:b], T[kind + "b"][:, a:b]).then_inc(sem.stored, 16)
+
+    store(g.sync, "y", [me], COLS)
+    store(g.sync, "z", [me], NC)
+    store(g.sync, "z", [near], NC)
+    store(g.sync, "y", [near], COLS)
+    store(g.sync, "z", list(range(lo, hi)), NC)
+    store(g.scalar, "y", list(range(lo, hi)), COLS)
+    g.sync.wait_ge(sem.stored, 6 * 16)

@@ -1,7 +1,8 @@
+import numpy as np
 from concourse.bass import DstId, RemoteDMATransfer
 from concourse.mybir import dt, AluOpType, ActivationFunctionType
 
-C = 0.019
+C = float(np.float32(0.019))
 N, COLS, NC = 4, 128, 256
 
 SCRATCH = {
@@ -23,8 +24,9 @@ SCRATCH = {
     "zb": ("sbuf", [128, N * NC], "float32"),
     "ps": ("psum", [128, 512 * 8], "float32"),
 }
-SEMAPHORES = (["ld_" + k for k in "xeawv"] + ["q_" + k for k in "xeawvt"] + ["u0", "u1", "d0", "d1", "k0", "k1", "k2", "k3", "res"]
-              + ["py%d" % j for j in range(N)] + ["pz%d" % j for j in range(N)]
+SEMAPHORES = (["ld_" + k for k in "xeawv"] + ["q_" + k for k in ("x", "e", "a0", "a1", "w", "v", "t")]
+              + ["u0", "u1", "d0", "d1", "k0", "k1", "k2", "k3", "res"]
+              + ["py%d" % j for j in range(N)] + ["pz%d" % j for j in range(N)] + ["ph"]
               + ["cy%d" % j for j in range(N)] + ["cz%d" % j for j in range(N)]
               + ["arr%d" % j for j in range(N)] + ["sent", "stored"])
 
@@ -40,12 +42,12 @@ def rank_program(g, core, T, topo):
     if me is None:
         return
     sem = T.sem
-    copy = ActivationFunctionType.Copy
+    act = ActivationFunctionType
     near = [r for r in range(N) if r != me and topo.chip(T.cores[r]) == topo.chip(core)][0]
     far = [r for r in range(N) if topo.chip(T.cores[r]) != topo.chip(core)]
     far = sorted(far, key=lambda r: topo.die(T.cores[r]) != topo.die(core))
     f1, f2 = far
-    lo, hi = min(far), max(far) + 1
+    both = list(range(min(far), max(far) + 1))
     off = topo.mask(core, T.cores[f1])
     inner = topo.mask(core, T.cores[near]) & ~off
     n_off, n_in = 8, 4
@@ -54,39 +56,45 @@ def rank_program(g, core, T, topo):
     def cols(j, w=COLS):
         return slice(w * j, w * j + w)
 
-    def bank(k, n):
+    def bank(k, n=COLS):
         return T.ps[:, 512 * k:512 * k + n]
 
     g.scalar.dma_start(T.ab[:], T.a[:]).then_inc(sem.ld_a, 16)
     for k in "xewv":
         g.sync.dma_start(T[k + "b"][:], T[k][:]).then_inc(sem["ld_" + k], 16)
 
+    U, D = (0, 1), (2, 3)
+    ybank = {me: 4, near: 6, f1: 0, f2: 2}
+    zbank = {me: 5, near: 7, f1: 1, f2: 3}
+
     v = g.vector
+    part = {
+        "x": (T.xb[:], T.xq[:], T.xs[:]),
+        "e": (T.eb[:], T.eq[:], T.es[:]),
+        "a0": (T.ab[:, cols(0, 512)], T.aq[:, cols(0)], T.as_[:, cols(0)]),
+        "a1": (T.ab[:, cols(1, 512)], T.aq[:, cols(1)], T.as_[:, cols(1)]),
+        "w": (T.wb[:], T.wq[:], T.ws[:]),
+        "v": (T.vb[:], T.vq[:], T.vs[:]),
+    }
 
-    def quant(k, plane):
-        v.wait_ge(sem["ld_" + k], 16)
-        v.quantize_mx(T[k + "q"][:], T[plane][:], T[k + "b"][:]).then_inc(sem["q_" + k], 1)
+    def quant(k):
+        v.wait_ge(sem["ld_" + k[0]], 16)
+        v.quantize_mx(part[k][1], part[k][2], part[k][0]).then_inc(sem["q_" + k], 1)
 
-    def masks(i):
-        v.wait_ge(sem["u%d" % i], 1)
-        for h, op in enumerate((AluOpType.is_gt, AluOpType.is_lt)):
-            b = 2 * i + h
-            v.tensor_scalar(T["m%d" % b][:], bank(i, COLS), 0.0, C, op, AluOpType.mult).then_inc(sem["k%d" % b], 1)
-
-    quant("x", "xs")
-    quant("a", "as_")
-    masks(0)
-    quant("e", "es")
-    masks(1)
-    for i in range(2):
-        v.wait_ge(sem["d%d" % i], 1)
-        for b in (2 * i, 2 * i + 1):
-            v.wait_ge(sem["k%d" % b], 1)
-            v.tensor_tensor(T.tb[:, b:4 * COLS:4], T["m%d" % b][:], bank(2 + i, COLS), AluOpType.mult).then_inc(sem.res, 1)
+    for k in ("x", "a0", "a1", "e"):
+        quant(k)
+    for b in range(4):
+        v.wait_ge(sem["u%d" % (b // 2)], 1)
+        op = AluOpType.is_lt if b % 2 else AluOpType.is_gt
+        v.tensor_scalar(T["m%d" % b][:], bank(U[b // 2]), 0.0, C, op, AluOpType.mult).then_inc(sem["k%d" % b], 1)
+    for b in range(4):
+        v.wait_ge(sem["d%d" % (b // 2)], 1)
+        v.wait_ge(sem["k%d" % b], 1)
+        v.tensor_tensor(T.tb[:, b:4 * COLS:4], T["m%d" % b][:], bank(D[b // 2]), AluOpType.mult).then_inc(sem.res, 1)
     v.wait_ge(sem.res, 4)
     v.quantize_mx(T.q[:, cols(me)], T.s[:, cols(me)], T.tb[:]).then_inc(sem.q_t, 1)
-    quant("w", "ws")
-    quant("v", "vs")
+    quant("w")
+    quant("v")
 
     g.wait_ge(sem.q_t, 1)
 
@@ -95,71 +103,82 @@ def rank_program(g, core, T, topo):
         return DstId(rid=rid, pnc=pnc)
 
     arr = sem["arr%d" % me]
-    for part in (T.q[:, cols(me)].bitcast(dt.uint8), T.s[:, cols(me)]):
+    for p in (T.q[:, cols(me)].bitcast(dt.uint8), T.s[:, cols(me)]):
         g.remote_dma_fused([
-            RemoteDMATransfer(dst_ids=[dst(f1), dst(f2)], dma_engine_mask=m_off, remote_sem=arr, srcs=[part], dsts=[part, part]),
-            RemoteDMATransfer(dst_ids=[dst(near)], dma_engine_mask=m_in, remote_sem=arr, srcs=[part], dsts=[part]),
+            RemoteDMATransfer(dst_ids=[dst(f1), dst(f2)], dma_engine_mask=m_off, remote_sem=arr, srcs=[p], dsts=[p, p]),
+            RemoteDMATransfer(dst_ids=[dst(near)], dma_engine_mask=m_in, remote_sem=arr, srcs=[p], dsts=[p]),
         ], local_sem=sem.sent)
     g.wait_ge(sem.sent, 2 * (n_off + n_in))
 
     t = g.tensor
 
-    def yprod(j, k):
-        t.matmul_mx(bank(k, COLS), T.wq[:], T.ws[:], T.q[:, cols(j)], T.s[:, cols(j)], True, True).then_inc(sem["py%d" % j], 1)
+    def tprod(k, i, key, name):
+        t.matmul_mx(bank(k), part["a%d" % i][1], part["a%d" % i][2], part[key][1], part[key][2], True, True).then_inc(sem[name], 1)
 
-    def zprod(j, k):
-        t.matmul_mx(bank(k, NC), T.q[:, cols(j)], T.s[:, cols(j)], T.vq[:], T.vs[:], True, True).then_inc(sem["pz%d" % j], 1)
+    def yprod(j):
+        t.matmul_mx(bank(ybank[j]), T.wq[:], T.ws[:], T.q[:, cols(j)], T.s[:, cols(j)], True, True).then_inc(sem["py%d" % j], 1)
+
+    def zprod(j, k, a, b, name):
+        t.matmul_mx(bank(k, b - a), T.q[:, cols(j)], T.s[:, cols(j)], T.vq[:, a:b], T.vs[:, a:b], True, True).then_inc(sem[name], 1)
 
     t.wait_ge(sem.q_x, 1)
-    t.wait_ge(sem.q_a, 1)
-    for i in range(2):
-        t.matmul_mx(bank(i, COLS), T.aq[:, cols(i)], T.as_[:, cols(i)], T.xq[:], T.xs[:], True, True).then_inc(sem["u%d" % i], 1)
+    t.wait_ge(sem.q_a0, 1)
+    tprod(U[0], 0, "x", "u0")
+    t.wait_ge(sem.q_a1, 1)
+    tprod(U[1], 1, "x", "u1")
     t.wait_ge(sem.q_e, 1)
-    for i in range(2):
-        t.matmul_mx(bank(2 + i, COLS), T.aq[:, cols(i)], T.as_[:, cols(i)], T.eq[:], T.es[:], True, True).then_inc(sem["d%d" % i], 1)
-    ybank = {me: 4, near: 6, f1: 0, f2: 2}
-    zbank = {me: 5, near: 7, f1: 1, f2: 3}
+    tprod(D[0], 0, "e", "d0")
+    tprod(D[1], 1, "e", "d1")
     t.wait_ge(sem.q_t, 1)
     t.wait_ge(sem.q_w, 1)
-    yprod(me, ybank[me])
+    yprod(me)
     t.wait_ge(sem.q_v, 1)
-    zprod(me, zbank[me])
+    zprod(me, zbank[me], 0, NC, "pz%d" % me)
     t.wait_ge(sem["arr%d" % near], 2 * n_in)
-    zprod(near, zbank[near])
-    yprod(near, ybank[near])
-    for j in far:
-        t.wait_ge(sem["arr%d" % j], 2 * n_off)
-        zprod(j, zbank[j])
-    for j in far:
-        yprod(j, ybank[j])
+    zprod(near, zbank[near], 0, NC, "pz%d" % near)
+    yprod(near)
+    t.wait_ge(sem["arr%d" % f1], 2 * n_off)
+    zprod(f1, zbank[f1], 0, NC, "pz%d" % f1)
+    yprod(f1)
+    t.wait_ge(sem["cy%d" % me], 1)
+    t.wait_ge(sem["arr%d" % f2], 2 * n_off)
+    zprod(f2, zbank[f2], 0, NC // 2, "pz%d" % f2)
+    zprod(f2, ybank[me], NC // 2, NC, "ph")
+    yprod(f2)
 
-    def out_v(kind, j, k, w):
-        v.wait_ge(sem["p%s%d" % (kind, j)], 1)
-        v.tensor_copy(T[kind + "b"][:, cols(j, w)], bank(k, w)).then_inc(sem["c%s%d" % (kind, j)], 1)
+    def out(queue, src, to, ready, done):
+        queue.wait_ge(sem[ready], 1)
+        i = v.tensor_copy(to, src) if queue is v else g.scalar.activation(to, src, act.Copy)
+        i.then_inc(sem[done], 1)
 
-    def out_s(kind, j, k, w):
-        g.scalar.wait_ge(sem["p%s%d" % (kind, j)], 1)
-        g.scalar.activation(T[kind + "b"][:, cols(j, w)], bank(k, w), copy).then_inc(sem["c%s%d" % (kind, j)], 1)
+    def out_y(queue, j):
+        out(queue, bank(ybank[j]), T.yb[:, cols(j)], "py%d" % j, "cy%d" % j)
 
-    out_v("y", me, ybank[me], COLS)
-    out_s("z", me, zbank[me], NC)
-    out_v("z", near, zbank[near], NC)
-    out_s("y", near, ybank[near], COLS)
-    out_v("z", f1, zbank[f1], NC)
-    out_s("z", f2, zbank[f2], NC)
-    out_v("y", f1, ybank[f1], COLS)
-    out_s("y", f2, ybank[f2], COLS)
+    def out_z(queue, j):
+        out(queue, bank(zbank[j], NC), T.zb[:, cols(j, NC)], "pz%d" % j, "cz%d" % j)
+
+    out_y(v, me)
+    out_z(g.scalar, me)
+    out_z(v, near)
+    out_y(v, near)
+    out_z(g.scalar, f1)
+    out_y(v, f1)
+    h = NC * f2 + NC // 2
+    out(v, bank(zbank[f2]), T.zb[:, NC * f2:h], "pz%d" % f2, "cz%d" % f2)
+    out(g.scalar, bank(ybank[me]), T.zb[:, h:NC * f2 + NC], "ph", "cz%d" % f2)
+    out_y(v, f2)
 
     def store(queue, kind, js, w):
         for j in js:
-            queue.wait_ge(sem["c%s%d" % (kind, j)], 1)
+            queue.wait_ge(sem["c%s%d" % (kind, j)], 2 if kind == "z" and j == f2 else 1)
         a, b = w * min(js), w * (max(js) + 1)
         queue.dma_start(T[kind][:, a:b], T[kind + "b"][:, a:b]).then_inc(sem.stored, 16)
 
+    g.sync.wait_ge(sem["arr%d" % near], 2 * n_in)
     store(g.sync, "y", [me], COLS)
     store(g.sync, "z", [me], NC)
     store(g.sync, "z", [near], NC)
     store(g.sync, "y", [near], COLS)
-    store(g.sync, "z", list(range(lo, hi)), NC)
-    store(g.scalar, "y", list(range(lo, hi)), COLS)
+    store(g.sync, "y", both, COLS)
+    store(g.scalar, "z", both, NC)
     g.sync.wait_ge(sem.stored, 6 * 16)

@@ -4,6 +4,7 @@ from concourse.mybir import dt, AluOpType, ActivationFunctionType
 
 C = float(np.float32(0.019))
 N, COLS, NC = 4, 128, 256
+H = COLS // 2
 
 SCRATCH = {
     "xb": ("sbuf", [128, 512], "bfloat16"),
@@ -11,12 +12,13 @@ SCRATCH = {
     "ab": ("sbuf", [128, 1024], "bfloat16"),
     "wb": ("sbuf", [128, 512], "bfloat16"),
     "vb": ("sbuf", [128, 1024], "bfloat16"),
-    "tb": ("sbuf", [128, 512], "bfloat16"),
+    "tb": ("sbuf", [128, 4 * 3 * H], "bfloat16"),
     "xq": ("sbuf", [128, 128], "float8_e4m3fn_x4"), "xs": ("sbuf", [128, 128], "uint8"),
     "eq": ("sbuf", [128, 128], "float8_e4m3fn_x4"), "es": ("sbuf", [128, 128], "uint8"),
     "aq": ("sbuf", [128, 256], "float8_e4m3fn_x4"), "as_": ("sbuf", [128, 256], "uint8"),
     "wq": ("sbuf", [128, 128], "float8_e4m3fn_x4"), "ws": ("sbuf", [128, 128], "uint8"),
     "vq": ("sbuf", [128, 256], "float8_e4m3fn_x4"), "vs": ("sbuf", [128, 256], "uint8"),
+    "ownq": ("sbuf", [128, 3 * H], "float8_e4m3fn_x4"), "owns": ("sbuf", [128, 3 * H], "uint8"),
     "q": ("sbuf", [128, N * COLS], "float8_e4m3fn_x4"), "s": ("sbuf", [128, N * COLS], "uint8"),
     "m0": ("sbuf", [128, 128], "float32"), "m1": ("sbuf", [128, 128], "float32"),
     "m2": ("sbuf", [128, 128], "float32"), "m3": ("sbuf", [128, 128], "float32"),
@@ -24,11 +26,9 @@ SCRATCH = {
     "zb": ("sbuf", [128, N * NC], "float32"),
     "ps": ("psum", [128, 512 * 8], "float32"),
 }
-SEMAPHORES = (["ld_" + k for k in "xeawv"] + ["q_" + k for k in ("x", "e", "a0", "a1", "w", "v", "t")]
-              + ["u0", "u1", "d0", "d1", "k0", "k1", "k2", "k3", "res"]
-              + ["py%d" % j for j in range(N)] + ["pz%d" % j for j in range(N)] + ["ph"]
-              + ["cy%d" % j for j in range(N)] + ["cz%d" % j for j in range(N)]
-              + ["arr%d" % j for j in range(N)] + ["sent", "stored"])
+SEMAPHORES = (["ld_" + k for k in "xeawv"] + ["q_" + k for k in ("x", "e", "a0", "a1", "w", "v", "ta", "tb")]
+              + ["u0", "u1", "d0", "d1", "zero", "res0", "res1"] + ["k%d%d" % (h, b) for h in (0, 1) for b in range(4)]
+              + ["%s%d" % (k, j) for k in ("py", "pz", "cy", "cz", "cod", "sca") for j in range(N)] + ["ph", "sent", "stored"])
 
 
 def engines(mask, n):
@@ -45,22 +45,21 @@ def rank_program(g, core, T, topo):
     act = ActivationFunctionType
     near = [r for r in range(N) if r != me and topo.chip(T.cores[r]) == topo.chip(core)][0]
     far = [r for r in range(N) if topo.chip(T.cores[r]) != topo.chip(core)]
-    far = sorted(far, key=lambda r: topo.die(T.cores[r]) != topo.die(core))
-    f1, f2 = far
-    both = list(range(min(far), max(far) + 1))
+    f1, f2 = sorted(far, key=lambda r: topo.die(T.cores[r]) != topo.die(core))
     off = topo.mask(core, T.cores[f1])
     inner = topo.mask(core, T.cores[near]) & ~off
-    n_off, n_in = 8, 4
+    n_off = n_in = 8
     m_off, m_in = engines(off, n_off), engines(inner, n_in)
 
     def cols(j, w=COLS):
         return slice(w * j, w * j + w)
 
-    def bank(k, n=COLS):
-        return T.ps[:, 512 * k:512 * k + n]
+    def bank(k, n=COLS, first=0):
+        return T.ps[:, 512 * k + first:512 * k + first + n]
 
-    g.scalar.dma_start(T.ab[:], T.a[:]).then_inc(sem.ld_a, 16)
-    for k in "xewv":
+    for k in "xaewv":
+        if k == "w":
+            g.sync.wait_ge(sem.ld_x, 16)
         g.sync.dma_start(T[k + "b"][:], T[k][:]).then_inc(sem["ld_" + k], 16)
 
     U, D = (0, 1), (2, 3)
@@ -81,45 +80,70 @@ def rank_program(g, core, T, topo):
         v.wait_ge(sem["ld_" + k[0]], 16)
         v.quantize_mx(part[k][1], part[k][2], part[k][0]).then_inc(sem["q_" + k], 1)
 
+    v.memset(T.tb[:, 4 * H:4 * 3 * H], 0.0).then_inc(sem.zero, 1)
     for k in ("x", "a0", "a1", "e"):
         quant(k)
-    for b in range(4):
-        v.wait_ge(sem["u%d" % (b // 2)], 1)
-        op = AluOpType.is_lt if b % 2 else AluOpType.is_gt
-        v.tensor_scalar(T["m%d" % b][:], bank(U[b // 2]), 0.0, C, op, AluOpType.mult).then_inc(sem["k%d" % b], 1)
-    for b in range(4):
-        v.wait_ge(sem["d%d" % (b // 2)], 1)
-        v.wait_ge(sem["k%d" % b], 1)
-        v.tensor_tensor(T.tb[:, b:4 * COLS:4], T["m%d" % b][:], bank(D[b // 2]), AluOpType.mult).then_inc(sem.res, 1)
-    v.wait_ge(sem.res, 4)
-    v.quantize_mx(T.q[:, cols(me)], T.s[:, cols(me)], T.tb[:]).then_inc(sem.q_t, 1)
+    for h in (0, 1):
+        for b in range(4):
+            v.wait_ge(sem["u%d" % (b // 2)], 1)
+            op = AluOpType.is_lt if b % 2 else AluOpType.is_gt
+            v.tensor_scalar(T["m%d" % b][:, cols(h, H)], bank(U[b // 2], H, H * h), 0.0, C, op, AluOpType.mult).then_inc(sem["k%d%d" % (h, b)], 1)
+        v.wait_ge(sem.q_ta if h else sem.zero, 1)
+        for b in range(4):
+            v.wait_ge(sem["d%d" % (b // 2)], 1)
+            v.wait_ge(sem["k%d%d" % (h, b)], 1)
+            v.tensor_tensor(T.tb[:, 4 * H * h + b:4 * H * (h + 1):4], T["m%d" % b][:, cols(h, H)], bank(D[b // 2], H, H * h),
+                            AluOpType.mult).then_inc(sem["res%d" % h], 1)
+        v.wait_ge(sem["res%d" % h], 4)
+        w = slice(H * h, H * (h + 2))
+        v.quantize_mx(T.ownq[:, w], T.owns[:, w], T.tb[:, 4 * H * h:4 * H * (h + 2)]).then_inc(sem.q_tb if h else sem.q_ta, 1)
     quant("w")
     quant("v")
-
-    g.wait_ge(sem.q_t, 1)
 
     def dst(r):
         rid, pnc, _ = topo.addr(T.cores[r])
         return DstId(rid=rid, pnc=pnc)
 
-    arr = sem["arr%d" % me]
-    for p in (T.q[:, cols(me)].bitcast(dt.uint8), T.s[:, cols(me)]):
-        g.remote_dma_fused([
-            RemoteDMATransfer(dst_ids=[dst(f1), dst(f2)], dma_engine_mask=m_off, remote_sem=arr, srcs=[p], dsts=[p, p]),
-            RemoteDMATransfer(dst_ids=[dst(near)], dma_engine_mask=m_in, remote_sem=arr, srcs=[p], dsts=[p]),
-        ], local_sem=sem.sent)
-    g.wait_ge(sem.sent, 2 * (n_off + n_in))
+    def codes(buf, a, b):
+        return T[buf][:, a:b].bitcast(dt.uint8)
+
+    def send(r, src, to, sm):
+        m = m_in if r == near else m_off
+        return RemoteDMATransfer(dst_ids=[dst(r)], dma_engine_mask=m, remote_sem=sem["%s%d" % sm], srcs=[src], dsts=[to])
+
+    def send_codes(r, a, b):
+        return send(r, codes("ownq", a, b), codes("q", COLS * me + a, COLS * me + b), ("cod", me))
+
+    def send_scales(r):
+        return send(r, T.owns[:, 0:COLS], T.s[:, cols(me)], ("sca", me))
+
+    g.wait_ge(sem.q_ta, 1)
+    g.remote_dma_fused([send_codes(f2, 0, H)], local_sem=sem.sent)
+    g.wait_ge(sem.q_tb, 1)
+    g.remote_dma_fused([send_scales(f1), send_scales(near)], local_sem=sem.sent)
+    g.remote_dma_fused([send_codes(f1, 0, COLS), send_codes(near, 0, COLS)], local_sem=sem.sent)
+    g.remote_dma_fused([send_codes(f2, H, COLS)], local_sem=sem.sent)
+    g.wait_ge(sem["sca%d" % f1], n_off)
+    g.remote_dma_fused([send(near, T.s[:, cols(f1)], T.s[:, cols(f1)], ("sca", f1))], local_sem=sem.sent)
+    g.wait_ge(sem.sent, 4 * n_off + 3 * n_in)
 
     t = g.tensor
+
+    def tile(j):
+        return (T.ownq[:, 0:COLS], T.owns[:, 0:COLS]) if j == me else (T.q[:, cols(j)], T.s[:, cols(j)])
 
     def tprod(k, i, key, name):
         t.matmul_mx(bank(k), part["a%d" % i][1], part["a%d" % i][2], part[key][1], part[key][2], True, True).then_inc(sem[name], 1)
 
     def yprod(j):
-        t.matmul_mx(bank(ybank[j]), T.wq[:], T.ws[:], T.q[:, cols(j)], T.s[:, cols(j)], True, True).then_inc(sem["py%d" % j], 1)
+        t.matmul_mx(bank(ybank[j]), T.wq[:], T.ws[:], tile(j)[0], tile(j)[1], True, True).then_inc(sem["py%d" % j], 1)
 
     def zprod(j, k, a, b, name):
-        t.matmul_mx(bank(k, b - a), T.q[:, cols(j)], T.s[:, cols(j)], T.vq[:, a:b], T.vs[:, a:b], True, True).then_inc(sem[name], 1)
+        t.matmul_mx(bank(k, b - a), tile(j)[0], tile(j)[1], T.vq[:, a:b], T.vs[:, a:b], True, True).then_inc(sem[name], 1)
+
+    def arrived(j):
+        t.wait_ge(sem["sca%d" % j], n_off if j == f1 else n_in)
+        t.wait_ge(sem["cod%d" % j], {near: n_in, f1: n_off, f2: 2 * n_off}[j])
 
     t.wait_ge(sem.q_x, 1)
     t.wait_ge(sem.q_a0, 1)
@@ -129,19 +153,17 @@ def rank_program(g, core, T, topo):
     t.wait_ge(sem.q_e, 1)
     tprod(D[0], 0, "e", "d0")
     tprod(D[1], 1, "e", "d1")
-    t.wait_ge(sem.q_t, 1)
+    t.wait_ge(sem.q_tb, 1)
     t.wait_ge(sem.q_w, 1)
     yprod(me)
     t.wait_ge(sem.q_v, 1)
     zprod(me, zbank[me], 0, NC, "pz%d" % me)
-    t.wait_ge(sem["arr%d" % near], 2 * n_in)
-    zprod(near, zbank[near], 0, NC, "pz%d" % near)
-    yprod(near)
-    t.wait_ge(sem["arr%d" % f1], 2 * n_off)
-    zprod(f1, zbank[f1], 0, NC, "pz%d" % f1)
-    yprod(f1)
+    for j in (near, f1):
+        arrived(j)
+        yprod(j)
+        zprod(j, zbank[j], 0, NC, "pz%d" % j)
     t.wait_ge(sem["cy%d" % me], 1)
-    t.wait_ge(sem["arr%d" % f2], 2 * n_off)
+    arrived(f2)
     zprod(f2, zbank[f2], 0, NC // 2, "pz%d" % f2)
     zprod(f2, ybank[me], NC // 2, NC, "ph")
     yprod(f2)
@@ -159,14 +181,14 @@ def rank_program(g, core, T, topo):
 
     out_y(v, me)
     out_z(g.scalar, me)
-    out_z(v, near)
     out_y(v, near)
-    out_z(g.scalar, f1)
+    out_z(g.scalar, near)
     out_y(v, f1)
+    out_z(v, f1)
     h = NC * f2 + NC // 2
-    out(v, bank(zbank[f2]), T.zb[:, NC * f2:h], "pz%d" % f2, "cz%d" % f2)
-    out(g.scalar, bank(ybank[me]), T.zb[:, h:NC * f2 + NC], "ph", "cz%d" % f2)
-    out_y(v, f2)
+    out(g.scalar, bank(zbank[f2]), T.zb[:, NC * f2:h], "pz%d" % f2, "cz%d" % f2)
+    out(v, bank(ybank[me]), T.zb[:, h:NC * f2 + NC], "ph", "cz%d" % f2)
+    out_y(g.scalar, f2)
 
     def store(queue, kind, js, w):
         for j in js:
@@ -174,11 +196,11 @@ def rank_program(g, core, T, topo):
         a, b = w * min(js), w * (max(js) + 1)
         queue.dma_start(T[kind][:, a:b], T[kind + "b"][:, a:b]).then_inc(sem.stored, 16)
 
-    g.sync.wait_ge(sem["arr%d" % near], 2 * n_in)
-    store(g.sync, "y", [me], COLS)
     store(g.sync, "z", [me], NC)
+    store(g.sync, "y", [me, near], COLS)
     store(g.sync, "z", [near], NC)
-    store(g.sync, "y", [near], COLS)
-    store(g.sync, "y", both, COLS)
-    store(g.scalar, "z", both, NC)
-    g.sync.wait_ge(sem.stored, 6 * 16)
+    store(g.sync, "y", [f1], COLS)
+    store(g.sync, "z", [f1], NC)
+    store(g.sync, "z", [f2], NC)
+    store(g.scalar, "y", [f2], COLS)
+    g.sync.wait_ge(sem.stored, 7 * 16)

import numpy as np
from concourse.bass import DstId, RemoteDMATransfer
from concourse.mybir import dt, AluOpType, ActivationFunctionType

C = float(np.float32(0.019))
N, COLS, NC = 4, 128, 256
H = COLS // 2

SCRATCH = {
    "xb": ("sbuf", [128, 512], "bfloat16"),
    "eb": ("sbuf", [128, 512], "bfloat16"),
    "ab": ("sbuf", [128, 1024], "bfloat16"),
    "wb": ("sbuf", [128, 512], "bfloat16"),
    "vb": ("sbuf", [128, 1024], "bfloat16"),
    "tb": ("sbuf", [128, 4 * 3 * H], "bfloat16"),
    "xq": ("sbuf", [128, 128], "float8_e4m3fn_x4"), "xs": ("sbuf", [128, 128], "uint8"),
    "eq": ("sbuf", [128, 128], "float8_e4m3fn_x4"), "es": ("sbuf", [128, 128], "uint8"),
    "aq": ("sbuf", [128, 256], "float8_e4m3fn_x4"), "as_": ("sbuf", [128, 256], "uint8"),
    "wq": ("sbuf", [128, 128], "float8_e4m3fn_x4"), "ws": ("sbuf", [128, 128], "uint8"),
    "vq": ("sbuf", [128, 256], "float8_e4m3fn_x4"), "vs": ("sbuf", [128, 256], "uint8"),
    "ownq": ("sbuf", [128, 3 * H], "float8_e4m3fn_x4"), "owns": ("sbuf", [128, 3 * H], "uint8"),
    "q": ("sbuf", [128, N * COLS], "float8_e4m3fn_x4"), "s": ("sbuf", [128, N * COLS], "uint8"),
    "m0": ("sbuf", [128, 128], "float32"), "m1": ("sbuf", [128, 128], "float32"),
    "m2": ("sbuf", [128, 128], "float32"), "m3": ("sbuf", [128, 128], "float32"),
    "yb": ("sbuf", [128, N * COLS], "float32"),
    "zb": ("sbuf", [128, N * NC], "float32"),
    "ps": ("psum", [128, 512 * 8], "float32"),
}
SEMAPHORES = (["ld_" + k for k in "xeawv"] + ["q_" + k for k in ("x", "e", "a0", "a1", "w", "v", "ta", "tb")]
              + ["u0", "u1", "d0", "d1", "zero", "res0", "res1"] + ["k%d%d" % (h, b) for h in (0, 1) for b in range(4)]
              + ["%s%d" % (k, j) for k in ("py", "pz", "cy", "cz", "cod", "sca") for j in range(N)] + ["ph", "sent", "stored"])


def engines(mask, n):
    bits = [b for b in range(mask.bit_length()) if mask >> b & 1]
    step = len(bits) // n
    return sum(1 << b for b in bits[::step][:n])


def rank_program(g, core, T, topo):
    me = T.rank_of(core)
    if me is None:
        return
    sem = T.sem
    act = ActivationFunctionType
    near = [r for r in range(N) if r != me and topo.chip(T.cores[r]) == topo.chip(core)][0]
    far = [r for r in range(N) if topo.chip(T.cores[r]) != topo.chip(core)]
    f1, f2 = sorted(far, key=lambda r: topo.die(T.cores[r]) != topo.die(core))
    off = topo.mask(core, T.cores[f1])
    inner = topo.mask(core, T.cores[near]) & ~off
    n_off = n_in = 8
    m_off, m_in = engines(off, n_off), engines(inner, n_in)

    def cols(j, w=COLS):
        return slice(w * j, w * j + w)

    def bank(k, n=COLS, first=0):
        return T.ps[:, 512 * k + first:512 * k + first + n]

    for k in "xaewv":
        if k == "w":
            g.sync.wait_ge(sem.ld_x, 16)
        g.sync.dma_start(T[k + "b"][:], T[k][:]).then_inc(sem["ld_" + k], 16)

    U, D = (0, 1), (2, 3)
    ybank = {me: 4, near: 6, f1: 0, f2: 2}
    zbank = {me: 5, near: 7, f1: 1, f2: 3}

    v = g.vector
    part = {
        "x": (T.xb[:], T.xq[:], T.xs[:]),
        "e": (T.eb[:], T.eq[:], T.es[:]),
        "a0": (T.ab[:, cols(0, 512)], T.aq[:, cols(0)], T.as_[:, cols(0)]),
        "a1": (T.ab[:, cols(1, 512)], T.aq[:, cols(1)], T.as_[:, cols(1)]),
        "w": (T.wb[:], T.wq[:], T.ws[:]),
        "v": (T.vb[:], T.vq[:], T.vs[:]),
    }

    def quant(k):
        v.wait_ge(sem["ld_" + k[0]], 16)
        v.quantize_mx(part[k][1], part[k][2], part[k][0]).then_inc(sem["q_" + k], 1)

    v.memset(T.tb[:, 4 * H:4 * 3 * H], 0.0).then_inc(sem.zero, 1)
    for k in ("x", "a0", "a1", "e"):
        quant(k)
    for h in (0, 1):
        for b in range(4):
            v.wait_ge(sem["u%d" % (b // 2)], 1)
            op = AluOpType.is_lt if b % 2 else AluOpType.is_gt
            v.tensor_scalar(T["m%d" % b][:, cols(h, H)], bank(U[b // 2], H, H * h), 0.0, C, op, AluOpType.mult).then_inc(sem["k%d%d" % (h, b)], 1)
        v.wait_ge(sem.q_ta if h else sem.zero, 1)
        for b in range(4):
            v.wait_ge(sem["d%d" % (b // 2)], 1)
            v.wait_ge(sem["k%d%d" % (h, b)], 1)
            v.tensor_tensor(T.tb[:, 4 * H * h + b:4 * H * (h + 1):4], T["m%d" % b][:, cols(h, H)], bank(D[b // 2], H, H * h),
                            AluOpType.mult).then_inc(sem["res%d" % h], 1)
        v.wait_ge(sem["res%d" % h], 4)
        w = slice(H * h, H * (h + 2))
        v.quantize_mx(T.ownq[:, w], T.owns[:, w], T.tb[:, 4 * H * h:4 * H * (h + 2)]).then_inc(sem.q_tb if h else sem.q_ta, 1)
    quant("w")
    quant("v")

    def dst(r):
        rid, pnc, _ = topo.addr(T.cores[r])
        return DstId(rid=rid, pnc=pnc)

    def codes(buf, a, b):
        return T[buf][:, a:b].bitcast(dt.uint8)

    def send(r, src, to, sm):
        m = m_in if r == near else m_off
        return RemoteDMATransfer(dst_ids=[dst(r)], dma_engine_mask=m, remote_sem=sem["%s%d" % sm], srcs=[src], dsts=[to])

    def send_codes(r, a, b):
        return send(r, codes("ownq", a, b), codes("q", COLS * me + a, COLS * me + b), ("cod", me))

    def send_scales(r):
        return send(r, T.owns[:, 0:COLS], T.s[:, cols(me)], ("sca", me))

    g.wait_ge(sem.q_ta, 1)
    g.remote_dma_fused([send_codes(f2, 0, H)], local_sem=sem.sent)
    g.wait_ge(sem.q_tb, 1)
    g.remote_dma_fused([send_scales(f1), send_scales(near)], local_sem=sem.sent)
    g.remote_dma_fused([send_codes(f1, 0, COLS), send_codes(near, 0, COLS)], local_sem=sem.sent)
    g.remote_dma_fused([send_codes(f2, H, COLS)], local_sem=sem.sent)
    g.wait_ge(sem["sca%d" % f1], n_off)
    g.remote_dma_fused([send(near, T.s[:, cols(f1)], T.s[:, cols(f1)], ("sca", f1))], local_sem=sem.sent)
    g.wait_ge(sem.sent, 4 * n_off + 3 * n_in)

    t = g.tensor

    def tile(j):
        return (T.ownq[:, 0:COLS], T.owns[:, 0:COLS]) if j == me else (T.q[:, cols(j)], T.s[:, cols(j)])

    def tprod(k, i, key, name):
        t.matmul_mx(bank(k), part["a%d" % i][1], part["a%d" % i][2], part[key][1], part[key][2], True, True).then_inc(sem[name], 1)

    def yprod(j):
        t.matmul_mx(bank(ybank[j]), T.wq[:], T.ws[:], tile(j)[0], tile(j)[1], True, True).then_inc(sem["py%d" % j], 1)

    def zprod(j, k, a, b, name):
        t.matmul_mx(bank(k, b - a), tile(j)[0], tile(j)[1], T.vq[:, a:b], T.vs[:, a:b], True, True).then_inc(sem[name], 1)

    def arrived(j):
        t.wait_ge(sem["sca%d" % j], n_off if j == f1 else n_in)
        t.wait_ge(sem["cod%d" % j], {near: n_in, f1: n_off, f2: 2 * n_off}[j])

    t.wait_ge(sem.q_x, 1)
    t.wait_ge(sem.q_a0, 1)
    tprod(U[0], 0, "x", "u0")
    t.wait_ge(sem.q_a1, 1)
    tprod(U[1], 1, "x", "u1")
    t.wait_ge(sem.q_e, 1)
    tprod(D[0], 0, "e", "d0")
    tprod(D[1], 1, "e", "d1")
    t.wait_ge(sem.q_tb, 1)
    t.wait_ge(sem.q_w, 1)
    yprod(me)
    t.wait_ge(sem.q_v, 1)
    zprod(me, zbank[me], 0, NC, "pz%d" % me)
    for j in (near, f1):
        arrived(j)
        yprod(j)
        zprod(j, zbank[j], 0, NC, "pz%d" % j)
    t.wait_ge(sem["cy%d" % me], 1)
    arrived(f2)
    zprod(f2, zbank[f2], 0, NC // 2, "pz%d" % f2)
    zprod(f2, ybank[me], NC // 2, NC, "ph")
    yprod(f2)

    def out(queue, src, to, ready, done):
        queue.wait_ge(sem[ready], 1)
        i = v.tensor_copy(to, src) if queue is v else g.scalar.activation(to, src, act.Copy)
        i.then_inc(sem[done], 1)

    def out_y(queue, j):
        out(queue, bank(ybank[j]), T.yb[:, cols(j)], "py%d" % j, "cy%d" % j)

    def out_z(queue, j):
        out(queue, bank(zbank[j], NC), T.zb[:, cols(j, NC)], "pz%d" % j, "cz%d" % j)

    out_y(v, me)
    out_z(g.scalar, me)
    out_y(v, near)
    out_z(g.scalar, near)
    out_y(v, f1)
    out_z(v, f1)
    h = NC * f2 + NC // 2
    out(g.scalar, bank(zbank[f2]), T.zb[:, NC * f2:h], "pz%d" % f2, "cz%d" % f2)
    out(v, bank(ybank[me]), T.zb[:, h:NC * f2 + NC], "ph", "cz%d" % f2)
    out_y(g.scalar, f2)

    def store(queue, kind, js, w):
        for j in js:
            queue.wait_ge(sem["c%s%d" % (kind, j)], 2 if kind == "z" and j == f2 else 1)
        a, b = w * min(js), w * (max(js) + 1)
        queue.dma_start(T[kind][:, a:b], T[kind + "b"][:, a:b]).then_inc(sem.stored, 16)

    store(g.sync, "z", [me], NC)
    store(g.sync, "y", [me, near], COLS)
    store(g.sync, "z", [near], NC)
    store(g.sync, "y", [f1], COLS)
    store(g.sync, "z", [f1], NC)
    store(g.sync, "z", [f2], NC)
    store(g.scalar, "y", [f2], COLS)
    g.sync.wait_ge(sem.stored, 7 * 16)
